import numpy as np
import ml_dtypes


def mxq(x, axis, fmt="e4m3"):
    dtype, down = {"e4m3": (ml_dtypes.float8_e4m3fn, 7), "e5m2": (ml_dtypes.float8_e5m2, 14)}[fmt]
    v = np.moveaxis(np.asarray(x, np.float32).astype(ml_dtypes.bfloat16).astype(np.float64), axis, -1)
    blocks = v.reshape(v.shape[:-1] + (-1, 32))
    amax = np.abs(blocks).max(-1, keepdims=True)
    byte = np.maximum(np.where(amax > 0, np.frexp(amax)[1] - 1 + 127, 0) - down, 1)
    scale = np.exp2(byte - 127.0)
    codes = (blocks / scale).astype(np.float32).astype(dtype).astype(np.float64)
    return np.moveaxis((codes * scale).reshape(v.shape), -1, axis)


WIDE = False


def mx_kscale(k):
    if not WIDE:
        return np.ones(k)
    levels = np.array([10, -10, 5, -5, 0])
    if k % 512:
        return np.exp2(np.random.permutation(np.resize(levels, k // 32))).repeat(32)
    a = np.empty((k // 512, 16))
    for p in range(k // 512):
        a[p, :8] = np.random.permutation(np.resize(levels, 8))
        for g in range(8):
            far = levels[np.abs(levels - a[p, g]) >= 10]
            a[p, g + 8] = far[np.random.randint(len(far))]
    return np.exp2(a.ravel()).repeat(32)


def f64(x):
    return np.asarray(x).astype(np.float64)


def striped8(idx):
    return np.asarray(idx).reshape(8, -1, 16).transpose(0, 2, 1).reshape(128, -1).astype(np.uint16)


def unstriped8(offs):
    return offs.reshape(8, 16, -1).transpose(0, 2, 1).reshape(8, -1).astype(np.int64)


def pick8(x, idx, run):
    r = np.arange(len(x))
    return x[r[:, None], idx[r % (8 * run) // run]]


D, T, I, Q, X, E, V, J = 512, 1024, 512, 256, 32, 512, 1024, 512


def setup_inputs():
    n = np.random.standard_normal
    idx = np.stack([np.random.permutation(T)[:I] for _ in range(8)])
    idx2 = np.stack([np.random.permutation(V)[:J] for _ in range(8)])
    fd = mx_kscale(D)
    fi = mx_kscale(I)
    fj = mx_kscale(J)
    ti = np.ones((8, T))
    np.put_along_axis(ti, idx, np.tile(fi, (8, 1)), axis=1)
    tj = np.ones((8, V))
    np.put_along_axis(tj, idx2, np.tile(fj, (8, 1)), axis=1)
    return {
        "query": (n((D, Q)) * (np.arange(D)[:, None] // 64 == np.arange(Q) % 8) * 0.0625 * fd[:, None]).astype(np.float32),
        "keys": (n((D, T)) / fd[:, None]).astype(np.float32),
        "rkey": (n((D, V)) / fd[:, None]).astype(np.float32),
        "size": (np.random.uniform(0.5, 2.0, (1, I)) * fi).astype(np.float32),
        "rsz": (np.random.uniform(0.5, 2.0, (1, J)) * fj).astype(np.float32),
        "vals": (n((E, T)) / ti[np.arange(E) % 512 // 64]).astype(np.float32),
        "rval": (n((E, V)) / tj[np.arange(E) % 512 // 64]).astype(np.float32),
        "own": ((np.arange(E)[:, None] // 64 == np.arange(Q) % 8) * 1.0).astype(np.float32),
        "offs": striped8(idx),
        "offs2": striped8(idx2),
    }


def reference(query, keys, rkey, size, rsz, vals, rval, own, offs, offs2):
    idx = unstriped8(offs)
    idx2 = unstriped8(offs2)
    queryq = mxq(f64(query), 0, "e4m3")
    keysidxq = mxq(pick8(f64(keys), idx, 64), 0, "e4m3")
    a = queryq.T @ keysidxq
    rkeyidx2q = mxq(pick8(f64(rkey), idx2, 64), 0, "e4m3")
    b = queryq.T @ rkeyidx2q
    m = np.maximum(np.max(a, axis=1, keepdims=True), np.max(b, axis=1, keepdims=True))
    p = np.exp(a - m)
    r = np.exp(b - m)
    z = np.sum(p, axis=1, keepdims=True) + np.sum(r, axis=1, keepdims=True)
    w = p * f64(size) / z
    u = r * f64(rsz) / z
    wt = w.T
    ut = u.T
    vt = pick8(f64(vals), idx, 64).T
    rt = pick8(f64(rval), idx2, 64).T
    vtq = mxq(vt, 0, "e4m3")
    wtq = mxq(wt, 0, "e4m3")
    rtq = mxq(rt, 0, "e4m3")
    utq = mxq(ut, 0, "e4m3")
    o = vtq.T @ wtq + rtq.T @ utq
    ob = o * f64(own)
    y = ob.reshape(E, X, Q // X).sum(axis=2)
    return y

@@ -1,0 +1,303 @@
+from contextlib import ExitStack
+
+import concourse.mybir as mybir
+from concourse.masks import make_identity
+
+D, T, SLOTS, Q, X, E = 512, 1024, 512, 256, 32, 512
+FLOPS = 2 * 2 * Q * D * SLOTS + 2 * 2 * E * SLOTS * Q
+
+F32 = mybir.dt.float32
+BF16 = mybir.dt.bfloat16
+I32 = mybir.dt.int32
+U32 = mybir.dt.uint32
+U16 = mybir.dt.uint16
+U8 = mybir.dt.uint8
+FP8X4 = mybir.dt.float8_e4m3fn_x4
+ACT = mybir.ActivationFunctionType
+ALU = mybir.AluOpType
+AXIS_X = mybir.AxisListType.X
+
+P = 128
+PACK = 4
+HALF = T // 2
+HEADS = Q // X
+SCALAR_PLANES = [(0, 0), (0, 1), (1, 0), (1, 2)]
+VECTOR_CASTS = [(0, 0, 1), (0, 1, 1), (1, 1, 1)]
+
+
+def tile_attend_ownlists_twopools_kernel(tc, query, keys, rkey, size, rsz, vals, rval, own, offs, offs2, out):
+    nc = tc.nc
+    key_pools = [keys.rearrange("(p t) c -> p t c", t=PACK), rkey.rearrange("(p t) c -> p t c", t=PACK)]
+    val_pools = [vals.rearrange("(p t) c -> p t c", t=PACK), rval.rearrange("(p t) c -> p t c", t=PACK)]
+
+    with ExitStack() as ctx:
+        keep = ctx.enter_context(tc.tile_pool(name="keep", bufs=1))
+        psum = ctx.enter_context(tc.psum_pool(name="psum", bufs=1))
+
+        def sb(name, shape, dtype, on=None):
+            return keep.tile(shape, dtype, name=name, tag=on or name, align_bytes=64)
+
+        def bank(name, tag, shape):
+            return psum.tile(shape, F32, name=name, tag=tag)
+
+        lists = [sb("list0", [P, SLOTS // 16], U16), sb("list1", [P, SLOTS // 16], U16)]
+        key_raw = {}
+        val_raw = {}
+
+        def load_keys(s, u):
+            for h in range(2):
+                key_raw[s, u, h] = sb("key_raw%d%d%d" % (s, u, h), [P, 2, HALF], F32)
+                nc.sync.dma_start(out=key_raw[s, u, h][:], in_=key_pools[s][:, 2 * u : 2 * u + 2, h * HALF : (h + 1) * HALF])
+
+        query_raw = sb("query_raw", [P, PACK, Q], F32)
+        nc.sync.dma_start(out=query_raw[:], in_=query.rearrange("(p t) q -> p t q", t=PACK))
+        nc.sync.dma_start(lists[0][:], offs)
+        load_keys(0, 0)
+        load_keys(0, 1)
+        nc.sync.dma_start(lists[1][:], offs2)
+        load_keys(1, 0)
+        weight_cols = []
+        for s, row in enumerate([size, rsz]):
+            weight_cols.append(sb("weight_cols%d" % s, [P, PACK], F32))
+            nc.sync.dma_start(out=weight_cols[s][:], in_=row.rearrange("o (n r) -> (o n) r", r=PACK))
+        load_keys(1, 1)
+        for s in range(2):
+            for t in range(PACK):
+                val_raw[s, t] = sb("val_raw%d%d" % (s, t), [P, T], F32)
+                nc.sync.dma_start(out=val_raw[s, t][:], in_=val_pools[s][:, t, :])
+        own_sb = sb("own_sb", [P, PACK, Q], F32)
+        nc.sync.dma_start(out=own_sb[:], in_=own.rearrange("(p t) q -> p t q", t=PACK))
+
+        ident = sb("ident", [P, P], F32)
+        make_identity(nc, ident[:])
+        warm = sb("warm", [P, 1], F32)
+        nc.scalar.activation(warm[:], ident[:, 0:1], ACT.Exp)
+
+        key_pairs = [sb("key_pairs%d" % s, [P, 2, SLOTS], U32) for s in range(2)]
+        key_window = {}
+
+        def cast_keys(s, u):
+            key_window[s, u] = sb("key_window%d%d" % (s, u), [P, T], U32)
+            as_pairs = key_window[s, u][:].bitcast(BF16).rearrange("p (c e) -> p c e", e=2)
+            for h in range(2):
+                dst = as_pairs[:, h * HALF : (h + 1) * HALF, :]
+                src = key_raw[s, u, h][:].rearrange("p e c -> p c e")
+                if (s, u, h) in VECTOR_CASTS:
+                    nc.vector.tensor_copy(dst, src)
+                else:
+                    nc.scalar.activation(dst, src, ACT.Copy)
+
+        def gather_keys(s, u):
+            nc.vector.tensor_copy(key_pairs[s][:, u, :], key_window[s, u][:].indirect(lists[s][:]))
+
+        def quantize(name, grouped, width):
+            codes = sb(name + "_codes", [P, width], U32)
+            scales = sb(name + "_scales", [P, width], U8)
+            nc.vector.quantize_mx(out=codes[:].bitcast(FP8X4), scales=scales[:], in_=grouped)
+            return codes, scales
+
+        key_grouped = {}
+
+        def group_keys(s):
+            key_grouped[s] = sb("key_grouped%d" % s, [P, SLOTS, 2], I32)
+            nc.vector.tensor_copy(key_grouped[s][:], key_pairs[s][:].bitcast(I32).rearrange("p u c -> p c u"))
+
+        scores = {}
+
+        def score(s):
+            k_codes, k_scales = quantize("key%d" % s, key_grouped[s][:].rearrange("p c u -> p (c u)").bitcast(BF16), SLOTS)
+            for j in range(2):
+                scores[s, j] = bank("scores%d%d" % (s, j), "bank%d" % (2 * s + j), [P, SLOTS])
+                cols = slice(j * P, (j + 1) * P)
+                nc.tensor.matmul_mx(
+                    out=scores[s, j][:],
+                    lhsT=q_codes[:, cols].bitcast(FP8X4),
+                    lhsT_scale=q_scales[:, cols],
+                    rhs=k_codes[:].bitcast(FP8X4),
+                    rhs_scale=k_scales[:],
+                    start=True,
+                    stop=True,
+                )
+
+        neg_max_first = {}
+        neg_max = {}
+        neg_scores = {}
+
+        def first_max(j, on=None):
+            neg_max_first[j] = sb("neg_max_first%d" % j, [P, 1], F32, on=on)
+            nc.vector.tensor_reduce(neg_max_first[j][:], scores[0, j][:], AXIS_X, ALU.max, negate=True)
+
+        def whole_max(j):
+            neg_max[j] = sb("neg_max%d" % j, [P, 1], F32)
+            neg_scores[j] = sb("neg_scores%d" % j, [P, SLOTS], F32)
+            nc.vector.tensor_scalar(neg_scores[j][:], scores[1, j][:], -1.0, neg_max_first[j][:], ALU.mult, ALU.min, accum_out=neg_max[j][:])
+
+        exps = {}
+        sums = {}
+
+        def exponentials(j):
+            sums[j] = sb("sums%d" % j, [P, 2], F32)
+            for s in range(2):
+                exps[s, j] = sb("exps%d%d" % (s, j), [P, SLOTS], F32)
+            nc.scalar.activation(exps[0, j][:], scores[0, j][:], ACT.Exp, bias=neg_max[j][:], accum_out=sums[j][:, 0:1])
+            nc.scalar.activation(exps[1, j][:], neg_scores[j][:], ACT.Exp, bias=neg_max[j][:], scale=-1.0, accum_out=sums[j][:, 1:2])
+
+        inverse = {}
+
+        def normaliser(j):
+            total = sb("total%d" % j, [P, 1], F32)
+            inverse[j] = sb("inverse%d" % j, [P, 1], F32)
+            nc.vector.tensor_tensor(total[:], sums[j][:, 0:1], sums[j][:, 1:2], ALU.add)
+            nc.vector.reciprocal(inverse[j][:], total[:])
+
+        w_turned = {}
+
+        def weights(s, j):
+            w = sb("w%d%d" % (s, j), [P, SLOTS], BF16)
+            nc.vector.scalar_tensor_tensor(
+                w[:].rearrange("p (n r) -> p n r", r=PACK),
+                exps[s, j][:].rearrange("p (n r) -> p n r", r=PACK),
+                inverse[j][:],
+                weight_rows[s][:].rearrange("p r n -> p n r"),
+                ALU.mult,
+                ALU.mult,
+            )
+            words = w[:].bitcast(F32)
+            if j == 0:
+                w_turned[s] = bank("w_turned%d" % s, "bank%d" % s, [P, 2, Q])
+            for u in range(2):
+                nc.tensor.transpose(w_turned[s][:, u, j * P : (j + 1) * P], words[:, u : SLOTS // 2 : 2], ident[:])
+
+        w_grouped = {}
+        w_mx = {}
+
+        def group_weights(s):
+            w_grouped[s] = sb("w_grouped%d" % s, [P, Q, 2], F32)
+            nc.scalar.copy(w_grouped[s][:], w_turned[s][:].rearrange("p u c -> p c u"))
+
+        def quantize_weights(s):
+            w_mx[s] = quantize("w%d" % s, w_grouped[s][:].rearrange("p c u -> p (c u)").bitcast(BF16), Q)
+
+        batches = {"a": [(0, 0), (0, 1)], "b": [(0, 2), (0, 3)], "c": [(1, 0), (1, 1)], "d": [(1, 2)], "e": [(1, 3)]}
+        batch_bank = {"a": 6, "b": 7, "c": 2, "d": 3, "e": 6}
+        batch_of = {plane: (b, i) for b in batches for i, plane in enumerate(batches[b])}
+        val_window = {}
+        val_turned = {}
+        val_grouped = {}
+        val_mx = {}
+
+        def cast_values(s, t):
+            val_window[s, t] = sb("val_window%d%d" % (s, t), [P, T], BF16)
+            nc.scalar.activation(val_window[s, t][:], val_raw[s, t][:], ACT.Copy)
+
+        def gather_values(s, t, on=None):
+            picked = sb("val_picked%d%d" % (s, t), [P, SLOTS], BF16, on=on)
+            if (s, t) in SCALAR_PLANES:
+                nc.scalar.activation(picked[:], val_window[s, t][:].indirect(lists[s][:]), ACT.Copy)
+            else:
+                nc.vector.tensor_copy(picked[:], val_raw[s, t][:].indirect(lists[s][:]))
+            words = picked[:].bitcast(F32)
+            b, i = batch_of[s, t]
+            if b not in val_turned:
+                val_turned[b] = bank("val_turned" + b, "bank%d" % batch_bank[b], [P, len(batches[b]), 2, P])
+            for u in range(2):
+                nc.tensor.transpose(val_turned[b][:, i, u, :], words[:, u : SLOTS // 2 : 2], ident[:])
+
+        def group_values(b):
+            val_grouped[b] = sb("val_grouped" + b, [P, len(batches[b]), P, 2], F32)
+            nc.scalar.copy(val_grouped[b][:], val_turned[b][:].rearrange("p n u c -> p n c u"))
+
+        def quantize_values(b):
+            codes, scales = quantize("val" + b, val_grouped[b][:].rearrange("p n c u -> p (n c u)").bitcast(BF16), len(batches[b]) * P)
+            for i, plane in enumerate(batches[b]):
+                val_mx[plane] = (codes[:, i * P : (i + 1) * P], scales[:, i * P : (i + 1) * P])
+
+        result = sb("result", [P, PACK, X], F32)
+        masked = {}
+
+        def product(t0, t1, bank_number):
+            acc = bank("acc%d" % t0, "bank%d" % bank_number, [P, t1 - t0, Q])
+            for t in range(t0, t1):
+                for s in range(2):
+                    nc.tensor.matmul_mx(
+                        out=acc[:, t - t0, :],
+                        lhsT=val_mx[s, t][0].bitcast(FP8X4),
+                        lhsT_scale=val_mx[s, t][1],
+                        rhs=w_mx[s][0][:].bitcast(FP8X4),
+                        rhs_scale=w_mx[s][1][:],
+                        start=(s == 0),
+                        stop=(s == 1),
+                    )
+            masked[t0] = sb("masked%d" % t0, [P, t1 - t0, Q], F32)
+            nc.vector.tensor_tensor(masked[t0][:], acc[:], own_sb[:, t0:t1, :], ALU.mult)
+
+        def head_sums(t0, t1):
+            nc.vector.tensor_reduce(result[:, t0:t1, :], masked[t0][:].rearrange("p t (x h) -> p t x h", h=HEADS), AXIS_X, ALU.add)
+
+        query_grouped = sb("query_grouped", [P, Q, PACK], BF16)
+        nc.vector.tensor_copy(query_grouped[:], query_raw[:].rearrange("p t q -> p q t"))
+        q_codes, q_scales = quantize("query", query_grouped[:].rearrange("p q t -> p (q t)"), Q)
+        cast_keys(0, 0)
+        gather_keys(0, 0)
+        cast_keys(0, 1)
+        gather_keys(0, 1)
+        group_keys(0)
+        cast_keys(1, 0)
+        score(0)
+        gather_keys(1, 0)
+
+        weight_rows = []
+        for s in range(2):
+            weight_rows.append(bank("weight_rows%d" % s, "bank%d" % (4 + s), [P, PACK, P]))
+            for r in range(PACK):
+                nc.tensor.transpose(weight_rows[s][:, r, :], weight_cols[s][:, r : r + 1].to_broadcast([P, P]), ident[:])
+
+        cast_keys(1, 1)
+        first_max(0, on="key_raw111")
+        gather_keys(1, 1)
+        first_max(1)
+        group_keys(1)
+        cast_values(0, 0)
+        gather_values(0, 0)
+        cast_values(0, 1)
+        gather_values(0, 1)
+        score(1)
+        gather_values(0, 2, on="key_grouped1")
+        whole_max(0)
+        whole_max(1)
+        group_values("a")
+        cast_values(1, 0)
+        exponentials(0)
+        exponentials(1)
+        gather_values(0, 3, on="neg_max_first1")
+        quantize_values("a")
+        normaliser(0)
+        weights(0, 0)
+        weights(1, 0)
+        normaliser(1)
+        gather_values(1, 0, on="neg_scores1")
+        group_values("b")
+        weights(0, 1)
+        weights(1, 1)
+        cast_values(1, 2)
+        gather_values(1, 1, on="exps11")
+        group_weights(0)
+        group_weights(1)
+        gather_values(1, 2)
+        quantize_values("b")
+        quantize_weights(0)
+        quantize_weights(1)
+        gather_values(1, 3, on="inverse1")
+        group_values("c")
+        group_values("d")
+        quantize_values("c")
+        group_values("e")
+        quantize_values("d")
+        product(0, 2, 4)
+        quantize_values("e")
+        head_sums(0, 2)
+        product(2, 3, 5)
+        product(3, 4, 7)
+        head_sums(2, 3)
+        head_sums(3, 4)
+        nc.sync.dma_start(out=out.rearrange("(p t) x -> p t x", t=PACK), in_=result[:])

@@ -19,10 +19,9 @@ AXIS_X = mybir.AxisListType.X
 
 P = 128
 PACK = 4
-HALF = T // 2
 HEADS = Q // X
-SCALAR_PLANES = [(0, 0), (0, 1), (1, 0), (1, 2)]
-VECTOR_CASTS = [(0, 0, 1), (0, 1, 1), (1, 1, 1)]
+SCALAR_PLANES = [(0, 0), (0, 1), (0, 2)]
+VECTOR_CAST_COLUMNS = [640, 256]
 
 
 def tile_attend_ownlists_twopools_kernel(tc, query, keys, rkey, size, rsz, vals, rval, own, offs, offs2, out):
@@ -45,26 +44,36 @@ def tile_attend_ownlists_twopools_kernel(tc, query, keys, rkey, size, rsz, vals,
         val_raw = {}
 
         def load_keys(s, u):
-            for h in range(2):
-                key_raw[s, u, h] = sb("key_raw%d%d%d" % (s, u, h), [P, 2, HALF], F32)
-                nc.sync.dma_start(out=key_raw[s, u, h][:], in_=key_pools[s][:, 2 * u : 2 * u + 2, h * HALF : (h + 1) * HALF])
+            key_raw[s, u] = sb("key_raw%d%d" % (s, u), [P, 2, T], F32)
+            nc.sync.dma_start(out=key_raw[s, u][:], in_=key_pools[s][:, 2 * u : 2 * u + 2, :])
 
+        def load_values(s, t, planes):
+            raw = sb("val_raw%d%d" % (s, t), [P, planes * T], F32)
+            nc.sync.dma_start(out=raw[:], in_=val_pools[s][:, t : t + planes, :].rearrange("p t c -> p (t c)"))
+            val_raw[s, t] = raw[:]
+            if planes == 2:
+                val_raw[s, t + 1] = raw[:, T:]
+
+        load_keys(0, 0)
+        nc.sync.dma_start(lists[0][:], offs)
+        load_keys(0, 1)
+        load_keys(1, 0)
+        load_keys(1, 1)
+        nc.sync.dma_start(lists[1][:], offs2)
         query_raw = sb("query_raw", [P, PACK, Q], F32)
         nc.sync.dma_start(out=query_raw[:], in_=query.rearrange("(p t) q -> p t q", t=PACK))
-        nc.sync.dma_start(lists[0][:], offs)
-        load_keys(0, 0)
-        load_keys(0, 1)
-        nc.sync.dma_start(lists[1][:], offs2)
-        load_keys(1, 0)
+        load_values(0, 0, 1)
         weight_cols = []
         for s, row in enumerate([size, rsz]):
             weight_cols.append(sb("weight_cols%d" % s, [P, PACK], F32))
             nc.sync.dma_start(out=weight_cols[s][:], in_=row.rearrange("o (n r) -> (o n) r", r=PACK))
-        load_keys(1, 1)
-        for s in range(2):
-            for t in range(PACK):
-                val_raw[s, t] = sb("val_raw%d%d" % (s, t), [P, T], F32)
-                nc.sync.dma_start(out=val_raw[s, t][:], in_=val_pools[s][:, t, :])
+        load_values(0, 1, 1)
+        load_values(0, 2, 1)
+        load_values(0, 3, 1)
+        load_values(1, 0, 1)
+        load_values(1, 1, 1)
+        load_values(1, 2, 1)
+        load_values(1, 3, 1)
         own_sb = sb("own_sb", [P, PACK, Q], F32)
         nc.sync.dma_start(out=own_sb[:], in_=own.rearrange("(p t) q -> p t q", t=PACK))
 
@@ -79,13 +88,10 @@ def tile_attend_ownlists_twopools_kernel(tc, query, keys, rkey, size, rsz, vals,
         def cast_keys(s, u):
             key_window[s, u] = sb("key_window%d%d" % (s, u), [P, T], U32)
             as_pairs = key_window[s, u][:].bitcast(BF16).rearrange("p (c e) -> p c e", e=2)
-            for h in range(2):
-                dst = as_pairs[:, h * HALF : (h + 1) * HALF, :]
-                src = key_raw[s, u, h][:].rearrange("p e c -> p c e")
-                if (s, u, h) in VECTOR_CASTS:
-                    nc.vector.tensor_copy(dst, src)
-                else:
-                    nc.scalar.activation(dst, src, ACT.Copy)
+            planes = key_raw[s, u][:].rearrange("p e c -> p c e")
+            split = VECTOR_CAST_COLUMNS[s]
+            nc.vector.tensor_copy(as_pairs[:, :split, :], planes[:, :split, :])
+            nc.scalar.activation(as_pairs[:, split:, :], planes[:, split:, :], ACT.Copy)
 
         def gather_keys(s, u):
             nc.vector.tensor_copy(key_pairs[s][:, u, :], key_window[s, u][:].indirect(lists[s][:]))
@@ -106,6 +112,7 @@ def tile_attend_ownlists_twopools_kernel(tc, query, keys, rkey, size, rsz, vals,
 
         def score(s):
             k_codes, k_scales = quantize("key%d" % s, key_grouped[s][:].rearrange("p c u -> p (c u)").bitcast(BF16), SLOTS)
+            q_codes, q_scales = q_mx
             for j in range(2):
                 scores[s, j] = bank("scores%d%d" % (s, j), "bank%d" % (2 * s + j), [P, SLOTS])
                 cols = slice(j * P, (j + 1) * P)
@@ -123,32 +130,28 @@ def tile_attend_ownlists_twopools_kernel(tc, query, keys, rkey, size, rsz, vals,
         neg_max = {}
         neg_scores = {}
 
-        def first_max(j, on=None):
-            neg_max_first[j] = sb("neg_max_first%d" % j, [P, 1], F32, on=on)
-            nc.vector.tensor_reduce(neg_max_first[j][:], scores[0, j][:], AXIS_X, ALU.max, negate=True)
+        def first_max(j):
+            neg_max_first[j] = sb("neg_max_first%d" % j, [P, 1], F32)
+            neg_scores[j] = sb("neg_scores%d" % j, [P, 2, SLOTS], F32)
+            nc.vector.tensor_scalar(neg_scores[j][:, 0, :], scores[0, j][:], -1.0, None, ALU.mult, ALU.min, accum_out=neg_max_first[j][:])
 
         def whole_max(j):
             neg_max[j] = sb("neg_max%d" % j, [P, 1], F32)
-            neg_scores[j] = sb("neg_scores%d" % j, [P, SLOTS], F32)
-            nc.vector.tensor_scalar(neg_scores[j][:], scores[1, j][:], -1.0, neg_max_first[j][:], ALU.mult, ALU.min, accum_out=neg_max[j][:])
+            nc.vector.tensor_scalar(neg_scores[j][:, 1, :], scores[1, j][:], -1.0, neg_max_first[j][:], ALU.mult, ALU.min, accum_out=neg_max[j][:])
 
         exps = {}
         sums = {}
 
         def exponentials(j):
-            sums[j] = sb("sums%d" % j, [P, 2], F32)
-            for s in range(2):
-                exps[s, j] = sb("exps%d%d" % (s, j), [P, SLOTS], F32)
-            nc.scalar.activation(exps[0, j][:], scores[0, j][:], ACT.Exp, bias=neg_max[j][:], accum_out=sums[j][:, 0:1])
-            nc.scalar.activation(exps[1, j][:], neg_scores[j][:], ACT.Exp, bias=neg_max[j][:], scale=-1.0, accum_out=sums[j][:, 1:2])
+            sums[j] = sb("sums%d" % j, [P, 1], F32)
+            exps[j] = sb("exps%d" % j, [P, 2, SLOTS], F32)
+            nc.scalar.activation(exps[j][:], neg_scores[j][:], ACT.Exp, bias=neg_max[j][:], scale=-1.0, accum_out=sums[j][:])
 
         inverse = {}
 
         def normaliser(j):
-            total = sb("total%d" % j, [P, 1], F32)
             inverse[j] = sb("inverse%d" % j, [P, 1], F32)
-            nc.vector.tensor_tensor(total[:], sums[j][:, 0:1], sums[j][:, 1:2], ALU.add)
-            nc.vector.reciprocal(inverse[j][:], total[:])
+            nc.vector.reciprocal(inverse[j][:], sums[j][:])
 
         w_turned = {}
 
@@ -156,7 +159,7 @@ def tile_attend_ownlists_twopools_kernel(tc, query, keys, rkey, size, rsz, vals,
             w = sb("w%d%d" % (s, j), [P, SLOTS], BF16)
             nc.vector.scalar_tensor_tensor(
                 w[:].rearrange("p (n r) -> p n r", r=PACK),
-                exps[s, j][:].rearrange("p (n r) -> p n r", r=PACK),
+                exps[j][:, s, :].rearrange("p (n r) -> p n r", r=PACK),
                 inverse[j][:],
                 weight_rows[s][:].rearrange("p r n -> p n r"),
                 ALU.mult,
@@ -178,24 +181,24 @@ def tile_attend_ownlists_twopools_kernel(tc, query, keys, rkey, size, rsz, vals,
         def quantize_weights(s):
             w_mx[s] = quantize("w%d" % s, w_grouped[s][:].rearrange("p c u -> p (c u)").bitcast(BF16), Q)
 
-        batches = {"a": [(0, 0), (0, 1)], "b": [(0, 2), (0, 3)], "c": [(1, 0), (1, 1)], "d": [(1, 2)], "e": [(1, 3)]}
-        batch_bank = {"a": 6, "b": 7, "c": 2, "d": 3, "e": 6}
+        batches = {"a": [(0, 0), (0, 1)], "b": [(0, 2), (0, 3)], "c": [(1, 0)], "f": [(1, 1)], "d": [(1, 2)], "e": [(1, 3)]}
+        batch_bank = {"a": 2, "b": 3, "c": 6, "f": 7, "d": 2, "e": 3}
         batch_of = {plane: (b, i) for b in batches for i, plane in enumerate(batches[b])}
         val_window = {}
         val_turned = {}
         val_grouped = {}
         val_mx = {}
 
-        def cast_values(s, t):
-            val_window[s, t] = sb("val_window%d%d" % (s, t), [P, T], BF16)
-            nc.scalar.activation(val_window[s, t][:], val_raw[s, t][:], ACT.Copy)
+        def cast_values(s, t, on=None):
+            val_window[s, t] = sb("val_window%d%d" % (s, t), [P, T], BF16, on=on)
+            nc.scalar.activation(val_window[s, t][:], val_raw[s, t], ACT.Copy)
 
         def gather_values(s, t, on=None):
             picked = sb("val_picked%d%d" % (s, t), [P, SLOTS], BF16, on=on)
             if (s, t) in SCALAR_PLANES:
                 nc.scalar.activation(picked[:], val_window[s, t][:].indirect(lists[s][:]), ACT.Copy)
             else:
-                nc.vector.tensor_copy(picked[:], val_raw[s, t][:].indirect(lists[s][:]))
+                nc.vector.tensor_copy(picked[:], val_raw[s, t].indirect(lists[s][:]))
             words = picked[:].bitcast(F32)
             b, i = batch_of[s, t]
             if b not in val_turned:
@@ -203,8 +206,8 @@ def tile_attend_ownlists_twopools_kernel(tc, query, keys, rkey, size, rsz, vals,
             for u in range(2):
                 nc.tensor.transpose(val_turned[b][:, i, u, :], words[:, u : SLOTS // 2 : 2], ident[:])
 
-        def group_values(b):
-            val_grouped[b] = sb("val_grouped" + b, [P, len(batches[b]), P, 2], F32)
+        def group_values(b, on=None):
+            val_grouped[b] = sb("val_grouped" + b, [P, len(batches[b]), P, 2], F32, on=on)
             nc.scalar.copy(val_grouped[b][:], val_turned[b][:].rearrange("p n u c -> p n c u"))
 
         def quantize_values(b):
@@ -234,70 +237,75 @@ def tile_attend_ownlists_twopools_kernel(tc, query, keys, rkey, size, rsz, vals,
         def head_sums(t0, t1):
             nc.vector.tensor_reduce(result[:, t0:t1, :], masked[t0][:].rearrange("p t (x h) -> p t x h", h=HEADS), AXIS_X, ALU.add)
 
-        query_grouped = sb("query_grouped", [P, Q, PACK], BF16)
-        nc.vector.tensor_copy(query_grouped[:], query_raw[:].rearrange("p t q -> p q t"))
-        q_codes, q_scales = quantize("query", query_grouped[:].rearrange("p q t -> p (q t)"), Q)
+        weight_rows = []
+
+        def spread_slot_weights():
+            for s in range(2):
+                weight_rows.append(bank("weight_rows%d" % s, "bank%d" % (4 + s), [P, PACK, P]))
+                for r in range(PACK):
+                    nc.tensor.transpose(weight_rows[s][:, r, :], weight_cols[s][:, r : r + 1].to_broadcast([P, P]), ident[:])
+
         cast_keys(0, 0)
         gather_keys(0, 0)
         cast_keys(0, 1)
         gather_keys(0, 1)
         group_keys(0)
         cast_keys(1, 0)
-        score(0)
         gather_keys(1, 0)
-
-        weight_rows = []
-        for s in range(2):
-            weight_rows.append(bank("weight_rows%d" % s, "bank%d" % (4 + s), [P, PACK, P]))
-            for r in range(PACK):
-                nc.tensor.transpose(weight_rows[s][:, r, :], weight_cols[s][:, r : r + 1].to_broadcast([P, P]), ident[:])
-
+        spread_slot_weights()
         cast_keys(1, 1)
-        first_max(0, on="key_raw111")
+        query_grouped = sb("query_grouped", [P, Q, PACK], BF16)
+        nc.vector.tensor_copy(query_grouped[:], query_raw[:].rearrange("p t q -> p q t"))
         gather_keys(1, 1)
-        first_max(1)
+        q_mx = quantize("query", query_grouped[:].rearrange("p q t -> p (q t)"), Q)
+        score(0)
         group_keys(1)
-        cast_values(0, 0)
-        gather_values(0, 0)
-        cast_values(0, 1)
-        gather_values(0, 1)
         score(1)
-        gather_values(0, 2, on="key_grouped1")
+        first_max(0)
         whole_max(0)
+        first_max(1)
         whole_max(1)
-        group_values("a")
-        cast_values(1, 0)
         exponentials(0)
         exponentials(1)
-        gather_values(0, 3, on="neg_max_first1")
-        quantize_values("a")
         normaliser(0)
         weights(0, 0)
         weights(1, 0)
         normaliser(1)
-        gather_values(1, 0, on="neg_scores1")
-        group_values("b")
         weights(0, 1)
         weights(1, 1)
-        cast_values(1, 2)
-        gather_values(1, 1, on="exps11")
         group_weights(0)
         group_weights(1)
-        gather_values(1, 2)
-        quantize_values("b")
         quantize_weights(0)
         quantize_weights(1)
-        gather_values(1, 3, on="inverse1")
-        group_values("c")
+        cast_values(0, 0)
+        gather_values(0, 0)
+        cast_values(0, 1)
+        gather_values(0, 1)
+        cast_values(0, 2, on="neg_max_first0")
+        gather_values(0, 2)
+        gather_values(0, 3, on="key_grouped1")
+        gather_values(1, 0, on="neg_scores0")
+        gather_values(1, 1, on="neg_scores1")
+        group_values("a")
+        gather_values(1, 2, on="exps1")
+        group_values("b", on="w11")
+        gather_values(1, 3, on="w_grouped0")
+        group_values("c", on="w01")
+        group_values("f")
         group_values("d")
-        quantize_values("c")
         group_values("e")
+        quantize_values("a")
+        quantize_values("b")
+        quantize_values("c")
+        quantize_values("f")
         quantize_values("d")
-        product(0, 2, 4)
         quantize_values("e")
-        head_sums(0, 2)
-        product(2, 3, 5)
-        product(3, 4, 7)
+        product(0, 1, 4)
+        product(1, 2, 5)
+        product(2, 3, 0)
+        product(3, 4, 1)
+        head_sums(0, 1)
+        head_sums(1, 2)
         head_sums(2, 3)
         head_sums(3, 4)
         nc.sync.dma_start(out=out.rearrange("(p t) x -> p t x", t=PACK), in_=result[:])

@@ -19,74 +19,83 @@ AXIS_X = mybir.AxisListType.X
 
 P = 128
 PACK = 4
+POOLS = 2
+Q_TILES = Q // P
 HEADS = Q // X
-SCALAR_PLANES = [(0, 0), (0, 1), (0, 2)]
+GROUP = 16
+RUN = 4
+
+SCALAR_VALUE_PLANES = 3
 VECTOR_CAST_COLUMNS = [640, 256]
+
+SLOT_WEIGHT_BANKS = [4, 5]
+OUTPUT_BANKS = [4, 5, 0, 1]
+VALUE_BANKS = [2, 3, 6, 7]
+VALUE_BATCHES = [[(0, 0), (0, 1)], [(0, 2), (0, 3)], [(1, 0)], [(1, 1)], [(1, 2)], [(1, 3)]]
 
 
 def tile_attend_ownlists_twopools_kernel(tc, query, keys, rkey, size, rsz, vals, rval, own, offs, offs2, out):
     nc = tc.nc
-    key_pools = [keys.rearrange("(p t) c -> p t c", t=PACK), rkey.rearrange("(p t) c -> p t c", t=PACK)]
-    val_pools = [vals.rearrange("(p t) c -> p t c", t=PACK), rval.rearrange("(p t) c -> p t c", t=PACK)]
+    key_pools = [pool.rearrange("(p t) c -> p t c", t=PACK) for pool in (keys, rkey)]
+    val_pools = [pool.rearrange("(p t) c -> p t c", t=PACK) for pool in (vals, rval)]
+    value_planes = [(s, t) for s in range(POOLS) for t in range(PACK)]
 
     with ExitStack() as ctx:
         keep = ctx.enter_context(tc.tile_pool(name="keep", bufs=1))
         psum = ctx.enter_context(tc.psum_pool(name="psum", bufs=1))
 
-        def sb(name, shape, dtype, on=None):
-            return keep.tile(shape, dtype, name=name, tag=on or name, align_bytes=64)
+        def sbuf(name, shape, dtype, reuses=None):
+            return keep.tile(shape, dtype, name=name, tag=reuses or name, align_bytes=64)
 
-        def bank(name, tag, shape):
-            return psum.tile(shape, F32, name=name, tag=tag)
+        def bank(name, number, shape):
+            return psum.tile(shape, F32, name=name, tag="bank%d" % number)
 
-        lists = [sb("list0", [P, SLOTS // 16], U16), sb("list1", [P, SLOTS // 16], U16)]
+        lists = [sbuf("list%d" % s, [P, SLOTS // GROUP], U16) for s in range(POOLS)]
         key_raw = {}
-        val_raw = {}
 
         def load_keys(s, u):
-            key_raw[s, u] = sb("key_raw%d%d" % (s, u), [P, 2, T], F32)
+            key_raw[s, u] = sbuf("key_raw%d%d" % (s, u), [P, 2, T], F32)
             nc.sync.dma_start(out=key_raw[s, u][:], in_=key_pools[s][:, 2 * u : 2 * u + 2, :])
 
-        def load_values(s, t, planes):
-            raw = sb("val_raw%d%d" % (s, t), [P, planes * T], F32)
-            nc.sync.dma_start(out=raw[:], in_=val_pools[s][:, t : t + planes, :].rearrange("p t c -> p (t c)"))
-            val_raw[s, t] = raw[:]
-            if planes == 2:
-                val_raw[s, t + 1] = raw[:, T:]
-
         load_keys(0, 0)
+        slot_weight = []
+        for s, row in enumerate([size, rsz]):
+            slot_weight.append(sbuf("slot_weight%d" % s, [P, PACK], F32))
+            nc.scalar.dma_start(out=slot_weight[s][:], in_=row.rearrange("o (n r) -> (o n) r", r=PACK))
         nc.sync.dma_start(lists[0][:], offs)
         load_keys(0, 1)
         load_keys(1, 0)
         load_keys(1, 1)
         nc.sync.dma_start(lists[1][:], offs2)
-        query_raw = sb("query_raw", [P, PACK, Q], F32)
+        query_raw = sbuf("query_raw", [P, PACK, Q], F32)
         nc.sync.dma_start(out=query_raw[:], in_=query.rearrange("(p t) q -> p t q", t=PACK))
-        load_values(0, 0, 1)
-        weight_cols = []
-        for s, row in enumerate([size, rsz]):
-            weight_cols.append(sb("weight_cols%d" % s, [P, PACK], F32))
-            nc.sync.dma_start(out=weight_cols[s][:], in_=row.rearrange("o (n r) -> (o n) r", r=PACK))
-        load_values(0, 1, 1)
-        load_values(0, 2, 1)
-        load_values(0, 3, 1)
-        load_values(1, 0, 1)
-        load_values(1, 1, 1)
-        load_values(1, 2, 1)
-        load_values(1, 3, 1)
-        own_sb = sb("own_sb", [P, PACK, Q], F32)
-        nc.sync.dma_start(out=own_sb[:], in_=own.rearrange("(p t) q -> p t q", t=PACK))
+        val_raw = {}
+        for s, t in value_planes:
+            val_raw[s, t] = sbuf("val_raw%d%d" % (s, t), [P, T], F32)
+            nc.sync.dma_start(out=val_raw[s, t][:], in_=val_pools[s][:, t, :])
+        own_planes = sbuf("own_planes", [P, PACK, Q], F32)
+        nc.sync.dma_start(out=own_planes[:], in_=own.rearrange("(p t) q -> p t q", t=PACK))
 
-        ident = sb("ident", [P, P], F32)
+        ident = sbuf("ident", [P, P], F32)
         make_identity(nc, ident[:])
-        warm = sb("warm", [P, 1], F32)
-        nc.scalar.activation(warm[:], ident[:, 0:1], ACT.Exp)
 
-        key_pairs = [sb("key_pairs%d" % s, [P, 2, SLOTS], U32) for s in range(2)]
+        def quantize(name, grouped, width):
+            codes = sbuf(name + "_codes", [P, width], U32)
+            scales = sbuf(name + "_scales", [P, width], U8)
+            nc.vector.quantize_mx(out=codes[:].bitcast(FP8X4), scales=scales[:], in_=grouped)
+            return codes, scales
+
+        def turn_slots(turned, source):
+            words = source[:].bitcast(F32)
+            for u in range(2):
+                nc.tensor.transpose(turned(u), words[:, u : SLOTS // 2 : 2], ident[:])
+
+        key_pairs = [sbuf("key_pairs%d" % s, [P, 2, SLOTS], U32) for s in range(POOLS)]
         key_window = {}
+        key_grouped = {}
 
         def cast_keys(s, u):
-            key_window[s, u] = sb("key_window%d%d" % (s, u), [P, T], U32)
+            key_window[s, u] = sbuf("key_window%d%d" % (s, u), [P, T], U32)
             as_pairs = key_window[s, u][:].bitcast(BF16).rearrange("p (c e) -> p c e", e=2)
             planes = key_raw[s, u][:].rearrange("p e c -> p c e")
             split = VECTOR_CAST_COLUMNS[s]
@@ -96,25 +105,16 @@ def tile_attend_ownlists_twopools_kernel(tc, query, keys, rkey, size, rsz, vals,
         def gather_keys(s, u):
             nc.vector.tensor_copy(key_pairs[s][:, u, :], key_window[s, u][:].indirect(lists[s][:]))
 
-        def quantize(name, grouped, width):
-            codes = sb(name + "_codes", [P, width], U32)
-            scales = sb(name + "_scales", [P, width], U8)
-            nc.vector.quantize_mx(out=codes[:].bitcast(FP8X4), scales=scales[:], in_=grouped)
-            return codes, scales
-
-        key_grouped = {}
-
         def group_keys(s):
-            key_grouped[s] = sb("key_grouped%d" % s, [P, SLOTS, 2], I32)
+            key_grouped[s] = sbuf("key_grouped%d" % s, [P, SLOTS, 2], I32)
             nc.vector.tensor_copy(key_grouped[s][:], key_pairs[s][:].bitcast(I32).rearrange("p u c -> p c u"))
 
         scores = {}
 
         def score(s):
             k_codes, k_scales = quantize("key%d" % s, key_grouped[s][:].rearrange("p c u -> p (c u)").bitcast(BF16), SLOTS)
-            q_codes, q_scales = q_mx
-            for j in range(2):
-                scores[s, j] = bank("scores%d%d" % (s, j), "bank%d" % (2 * s + j), [P, SLOTS])
+            for j in range(Q_TILES):
+                scores[s, j] = bank("scores%d%d" % (s, j), Q_TILES * s + j, [P, SLOTS])
                 cols = slice(j * P, (j + 1) * P)
                 nc.tensor.matmul_mx(
                     out=scores[s, j][:],
@@ -126,124 +126,13 @@ def tile_attend_ownlists_twopools_kernel(tc, query, keys, rkey, size, rsz, vals,
                     stop=True,
                 )
 
-        neg_max_first = {}
-        neg_max = {}
-        neg_scores = {}
-
-        def first_max(j):
-            neg_max_first[j] = sb("neg_max_first%d" % j, [P, 1], F32)
-            neg_scores[j] = sb("neg_scores%d" % j, [P, 2, SLOTS], F32)
-            nc.vector.tensor_scalar(neg_scores[j][:, 0, :], scores[0, j][:], -1.0, None, ALU.mult, ALU.min, accum_out=neg_max_first[j][:])
-
-        def whole_max(j):
-            neg_max[j] = sb("neg_max%d" % j, [P, 1], F32)
-            nc.vector.tensor_scalar(neg_scores[j][:, 1, :], scores[1, j][:], -1.0, neg_max_first[j][:], ALU.mult, ALU.min, accum_out=neg_max[j][:])
-
-        exps = {}
-        sums = {}
-
-        def exponentials(j):
-            sums[j] = sb("sums%d" % j, [P, 1], F32)
-            exps[j] = sb("exps%d" % j, [P, 2, SLOTS], F32)
-            nc.scalar.activation(exps[j][:], neg_scores[j][:], ACT.Exp, bias=neg_max[j][:], scale=-1.0, accum_out=sums[j][:])
-
-        inverse = {}
-
-        def normaliser(j):
-            inverse[j] = sb("inverse%d" % j, [P, 1], F32)
-            nc.vector.reciprocal(inverse[j][:], sums[j][:])
-
-        w_turned = {}
-
-        def weights(s, j):
-            w = sb("w%d%d" % (s, j), [P, SLOTS], BF16)
-            nc.vector.scalar_tensor_tensor(
-                w[:].rearrange("p (n r) -> p n r", r=PACK),
-                exps[j][:, s, :].rearrange("p (n r) -> p n r", r=PACK),
-                inverse[j][:],
-                weight_rows[s][:].rearrange("p r n -> p n r"),
-                ALU.mult,
-                ALU.mult,
-            )
-            words = w[:].bitcast(F32)
-            if j == 0:
-                w_turned[s] = bank("w_turned%d" % s, "bank%d" % s, [P, 2, Q])
-            for u in range(2):
-                nc.tensor.transpose(w_turned[s][:, u, j * P : (j + 1) * P], words[:, u : SLOTS // 2 : 2], ident[:])
-
-        w_grouped = {}
-        w_mx = {}
-
-        def group_weights(s):
-            w_grouped[s] = sb("w_grouped%d" % s, [P, Q, 2], F32)
-            nc.scalar.copy(w_grouped[s][:], w_turned[s][:].rearrange("p u c -> p c u"))
-
-        def quantize_weights(s):
-            w_mx[s] = quantize("w%d" % s, w_grouped[s][:].rearrange("p c u -> p (c u)").bitcast(BF16), Q)
-
-        batches = {"a": [(0, 0), (0, 1)], "b": [(0, 2), (0, 3)], "c": [(1, 0)], "f": [(1, 1)], "d": [(1, 2)], "e": [(1, 3)]}
-        batch_bank = {"a": 2, "b": 3, "c": 6, "f": 7, "d": 2, "e": 3}
-        batch_of = {plane: (b, i) for b in batches for i, plane in enumerate(batches[b])}
-        val_window = {}
-        val_turned = {}
-        val_grouped = {}
-        val_mx = {}
-
-        def cast_values(s, t, on=None):
-            val_window[s, t] = sb("val_window%d%d" % (s, t), [P, T], BF16, on=on)
-            nc.scalar.activation(val_window[s, t][:], val_raw[s, t], ACT.Copy)
-
-        def gather_values(s, t, on=None):
-            picked = sb("val_picked%d%d" % (s, t), [P, SLOTS], BF16, on=on)
-            if (s, t) in SCALAR_PLANES:
-                nc.scalar.activation(picked[:], val_window[s, t][:].indirect(lists[s][:]), ACT.Copy)
-            else:
-                nc.vector.tensor_copy(picked[:], val_raw[s, t].indirect(lists[s][:]))
-            words = picked[:].bitcast(F32)
-            b, i = batch_of[s, t]
-            if b not in val_turned:
-                val_turned[b] = bank("val_turned" + b, "bank%d" % batch_bank[b], [P, len(batches[b]), 2, P])
-            for u in range(2):
-                nc.tensor.transpose(val_turned[b][:, i, u, :], words[:, u : SLOTS // 2 : 2], ident[:])
-
-        def group_values(b, on=None):
-            val_grouped[b] = sb("val_grouped" + b, [P, len(batches[b]), P, 2], F32, on=on)
-            nc.scalar.copy(val_grouped[b][:], val_turned[b][:].rearrange("p n u c -> p n c u"))
-
-        def quantize_values(b):
-            codes, scales = quantize("val" + b, val_grouped[b][:].rearrange("p n c u -> p (n c u)").bitcast(BF16), len(batches[b]) * P)
-            for i, plane in enumerate(batches[b]):
-                val_mx[plane] = (codes[:, i * P : (i + 1) * P], scales[:, i * P : (i + 1) * P])
-
-        result = sb("result", [P, PACK, X], F32)
-        masked = {}
-
-        def product(t0, t1, bank_number):
-            acc = bank("acc%d" % t0, "bank%d" % bank_number, [P, t1 - t0, Q])
-            for t in range(t0, t1):
-                for s in range(2):
-                    nc.tensor.matmul_mx(
-                        out=acc[:, t - t0, :],
-                        lhsT=val_mx[s, t][0].bitcast(FP8X4),
-                        lhsT_scale=val_mx[s, t][1],
-                        rhs=w_mx[s][0][:].bitcast(FP8X4),
-                        rhs_scale=w_mx[s][1][:],
-                        start=(s == 0),
-                        stop=(s == 1),
-                    )
-            masked[t0] = sb("masked%d" % t0, [P, t1 - t0, Q], F32)
-            nc.vector.tensor_tensor(masked[t0][:], acc[:], own_sb[:, t0:t1, :], ALU.mult)
-
-        def head_sums(t0, t1):
-            nc.vector.tensor_reduce(result[:, t0:t1, :], masked[t0][:].rearrange("p t (x h) -> p t x h", h=HEADS), AXIS_X, ALU.add)
-
-        weight_rows = []
+        slot_weight_rows = []
 
         def spread_slot_weights():
-            for s in range(2):
-                weight_rows.append(bank("weight_rows%d" % s, "bank%d" % (4 + s), [P, PACK, P]))
+            for s in range(POOLS):
+                slot_weight_rows.append(bank("slot_weight_rows%d" % s, SLOT_WEIGHT_BANKS[s], [P, PACK, P]))
                 for r in range(PACK):
-                    nc.tensor.transpose(weight_rows[s][:, r, :], weight_cols[s][:, r : r + 1].to_broadcast([P, P]), ident[:])
+                    nc.tensor.transpose(slot_weight_rows[s][:, r, :], slot_weight[s][:, r : r + 1].to_broadcast([P, P]), ident[:])
 
         cast_keys(0, 0)
         gather_keys(0, 0)
@@ -254,58 +143,116 @@ def tile_attend_ownlists_twopools_kernel(tc, query, keys, rkey, size, rsz, vals,
         gather_keys(1, 0)
         spread_slot_weights()
         cast_keys(1, 1)
-        query_grouped = sb("query_grouped", [P, Q, PACK], BF16)
-        nc.vector.tensor_copy(query_grouped[:], query_raw[:].rearrange("p t q -> p q t"))
+        query_grouped = sbuf("query_grouped", [P, Q, PACK], BF16)
+        nc.vector.tensor_copy(
+            query_grouped[:].rearrange("p (c i) t -> p c t i", i=RUN), query_raw[:].rearrange("p t (c i) -> p c t i", i=RUN)
+        )
         gather_keys(1, 1)
-        q_mx = quantize("query", query_grouped[:].rearrange("p q t -> p (q t)"), Q)
+        q_codes, q_scales = quantize("query", query_grouped[:].rearrange("p q t -> p (q t)"), Q)
         score(0)
         group_keys(1)
         score(1)
-        first_max(0)
-        whole_max(0)
-        first_max(1)
-        whole_max(1)
-        exponentials(0)
-        exponentials(1)
-        normaliser(0)
-        weights(0, 0)
-        weights(1, 0)
-        normaliser(1)
-        weights(0, 1)
-        weights(1, 1)
-        group_weights(0)
-        group_weights(1)
-        quantize_weights(0)
-        quantize_weights(1)
-        cast_values(0, 0)
-        gather_values(0, 0)
-        cast_values(0, 1)
-        gather_values(0, 1)
-        cast_values(0, 2, on="neg_max_first0")
-        gather_values(0, 2)
-        gather_values(0, 3, on="key_grouped1")
-        gather_values(1, 0, on="neg_scores0")
-        gather_values(1, 1, on="neg_scores1")
-        group_values("a")
-        gather_values(1, 2, on="exps1")
-        group_values("b", on="w11")
-        gather_values(1, 3, on="w_grouped0")
-        group_values("c", on="w01")
-        group_values("f")
-        group_values("d")
-        group_values("e")
-        quantize_values("a")
-        quantize_values("b")
-        quantize_values("c")
-        quantize_values("f")
-        quantize_values("d")
-        quantize_values("e")
-        product(0, 1, 4)
-        product(1, 2, 5)
-        product(2, 3, 0)
-        product(3, 4, 1)
-        head_sums(0, 1)
-        head_sums(1, 2)
-        head_sums(2, 3)
-        head_sums(3, 4)
+
+        neg_scores = {}
+        neg_max_first = {}
+        neg_max = {}
+        for j in range(Q_TILES):
+            neg_max_first[j] = sbuf("neg_max_first%d" % j, [P, 1], F32)
+            neg_scores[j] = sbuf("neg_scores%d" % j, [P, POOLS, SLOTS], F32)
+            nc.vector.tensor_scalar(neg_scores[j][:, 0, :], scores[0, j][:], -1.0, None, ALU.mult, ALU.min, accum_out=neg_max_first[j][:])
+            neg_max[j] = sbuf("neg_max%d" % j, [P, 1], F32)
+            nc.vector.tensor_scalar(
+                neg_scores[j][:, 1, :], scores[1, j][:], -1.0, neg_max_first[j][:], ALU.mult, ALU.min, accum_out=neg_max[j][:]
+            )
+        exps = {}
+        row_sum = {}
+        for j in range(Q_TILES):
+            row_sum[j] = sbuf("row_sum%d" % j, [P, 1], F32)
+            exps[j] = sbuf("exps%d" % j, [P, POOLS, SLOTS], F32)
+            nc.scalar.activation(exps[j][:], neg_scores[j][:], ACT.Exp, bias=neg_max[j][:], scale=-1.0, accum_out=row_sum[j][:])
+
+        weights_turned = {}
+        for j in range(Q_TILES):
+            inverse = sbuf("inverse%d" % j, [P, 1], F32)
+            nc.vector.reciprocal(inverse[:], row_sum[j][:])
+            for s in range(POOLS):
+                weights = sbuf("weights%d%d" % (s, j), [P, SLOTS], BF16)
+                nc.vector.scalar_tensor_tensor(
+                    weights[:].rearrange("p (n r) -> p n r", r=PACK),
+                    exps[j][:, s, :].rearrange("p (n r) -> p n r", r=PACK),
+                    inverse[:],
+                    slot_weight_rows[s][:].rearrange("p r n -> p n r"),
+                    ALU.mult,
+                    ALU.mult,
+                )
+                if j == 0:
+                    weights_turned[s] = bank("weights_turned%d" % s, s, [P, 2, Q])
+                turn_slots(lambda u: weights_turned[s][:, u, j * P : (j + 1) * P], weights)
+        weights_grouped = {}
+        for s in range(POOLS):
+            weights_grouped[s] = sbuf("weights_grouped%d" % s, [P, Q, 2], F32)
+            nc.scalar.copy(weights_grouped[s][:], weights_turned[s][:].rearrange("p u c -> p c u"))
+        weights_mx = [
+            quantize("weights%d" % s, weights_grouped[s][:].rearrange("p c u -> p (c u)").bitcast(BF16), Q) for s in range(POOLS)
+        ]
+
+        vector_gather_reuses = ["key_grouped1", "neg_scores0", "neg_scores1", "exps1", "weights_grouped0"]
+        place_of = {plane: (b, i) for b, batch in enumerate(VALUE_BATCHES) for i, plane in enumerate(batch)}
+        val_turned = {}
+        val_grouped = {}
+
+        def gather_values(number):
+            s, t = value_planes[number]
+            name = "val_picked%d%d" % (s, t)
+            if number < SCALAR_VALUE_PLANES:
+                last = number == SCALAR_VALUE_PLANES - 1
+                window = sbuf("val_window%d%d" % (s, t), [P, T], BF16, reuses="neg_max_first0" if last else None)
+                nc.scalar.activation(window[:], val_raw[s, t][:], ACT.Copy)
+                picked = sbuf(name, [P, SLOTS], BF16)
+                nc.scalar.activation(picked[:], window[:].indirect(lists[s][:]), ACT.Copy)
+            else:
+                picked = sbuf(name, [P, SLOTS], BF16, reuses=vector_gather_reuses[number - SCALAR_VALUE_PLANES])
+                nc.vector.tensor_copy(picked[:], val_raw[s, t][:].indirect(lists[s][:]))
+            b, i = place_of[s, t]
+            if i == 0:
+                val_turned[b] = bank("val_turned%d" % b, VALUE_BANKS[b % len(VALUE_BANKS)], [P, len(VALUE_BATCHES[b]), 2, P])
+            turn_slots(lambda u: val_turned[b][:, i, u, :], picked)
+
+        grouped_reuses = {1: "weights11", 2: "weights01"}
+
+        def group_values(b):
+            val_grouped[b] = sbuf("val_grouped%d" % b, [P, len(VALUE_BATCHES[b]), P, 2], F32, reuses=grouped_reuses.get(b))
+            nc.scalar.copy(val_grouped[b][:], val_turned[b][:].rearrange("p n u c -> p n c u"))
+
+        for number, plane in enumerate(value_planes):
+            earlier_tenant = place_of[plane][0] - len(VALUE_BANKS)
+            if earlier_tenant >= 0:
+                group_values(earlier_tenant)
+            gather_values(number)
+        for b in range(len(VALUE_BATCHES) - len(VALUE_BANKS), len(VALUE_BATCHES)):
+            group_values(b)
+        val_mx = {}
+        for b, batch in enumerate(VALUE_BATCHES):
+            codes, scales = quantize("val%d" % b, val_grouped[b][:].rearrange("p n c u -> p (n c u)").bitcast(BF16), len(batch) * P)
+            for i, plane in enumerate(batch):
+                val_mx[plane] = (codes[:, i * P : (i + 1) * P], scales[:, i * P : (i + 1) * P])
+
+        result = sbuf("result", [P, PACK, X], F32)
+        masked = {}
+        for t in range(PACK):
+            acc = bank("acc%d" % t, OUTPUT_BANKS[t], [P, Q])
+            for s in range(POOLS):
+                nc.tensor.matmul_mx(
+                    out=acc[:],
+                    lhsT=val_mx[s, t][0].bitcast(FP8X4),
+                    lhsT_scale=val_mx[s, t][1],
+                    rhs=weights_mx[s][0][:].bitcast(FP8X4),
+                    rhs_scale=weights_mx[s][1][:],
+                    start=(s == 0),
+                    stop=(s == POOLS - 1),
+                )
+            masked[t] = sbuf("masked%d" % t, [P, Q], F32)
+            nc.vector.tensor_tensor(masked[t][:], acc[:], own_planes[:, t, :], ALU.mult)
+        for t in range(PACK):
+            nc.vector.tensor_reduce(result[:, t, :], masked[t][:].rearrange("p (x h) -> p x h", h=HEADS), AXIS_X, ALU.add)
         nc.sync.dma_start(out=out.rearrange("(p t) x -> p t x", t=PACK), in_=result[:])

from contextlib import ExitStack

import concourse.mybir as mybir
from concourse.masks import make_identity

D, T, SLOTS, Q, X, E = 512, 1024, 512, 256, 32, 512
FLOPS = 2 * 2 * Q * D * SLOTS + 2 * 2 * E * SLOTS * Q

F32 = mybir.dt.float32
BF16 = mybir.dt.bfloat16
I32 = mybir.dt.int32
U32 = mybir.dt.uint32
U16 = mybir.dt.uint16
U8 = mybir.dt.uint8
FP8X4 = mybir.dt.float8_e4m3fn_x4
ACT = mybir.ActivationFunctionType
ALU = mybir.AluOpType
AXIS_X = mybir.AxisListType.X

P = 128
PACK = 4
POOLS = 2
Q_TILES = Q // P
HEADS = Q // X
GROUP = 16
RUN = 4

SCALAR_VALUE_PLANES = 3
VECTOR_CAST_COLUMNS = [640, 256]

SLOT_WEIGHT_BANKS = [4, 5]
OUTPUT_BANKS = [4, 5, 0, 1]
VALUE_BANKS = [2, 3, 6, 7]
VALUE_BATCHES = [[(0, 0), (0, 1)], [(0, 2), (0, 3)], [(1, 0)], [(1, 1)], [(1, 2)], [(1, 3)]]


def tile_attend_ownlists_twopools_kernel(tc, query, keys, rkey, size, rsz, vals, rval, own, offs, offs2, out):
    nc = tc.nc
    key_pools = [pool.rearrange("(p t) c -> p t c", t=PACK) for pool in (keys, rkey)]
    val_pools = [pool.rearrange("(p t) c -> p t c", t=PACK) for pool in (vals, rval)]
    value_planes = [(s, t) for s in range(POOLS) for t in range(PACK)]

    with ExitStack() as ctx:
        keep = ctx.enter_context(tc.tile_pool(name="keep", bufs=1))
        psum = ctx.enter_context(tc.psum_pool(name="psum", bufs=1))

        def sbuf(name, shape, dtype, reuses=None):
            return keep.tile(shape, dtype, name=name, tag=reuses or name, align_bytes=64)

        def bank(name, number, shape):
            return psum.tile(shape, F32, name=name, tag="bank%d" % number)

        lists = [sbuf("list%d" % s, [P, SLOTS // GROUP], U16) for s in range(POOLS)]
        key_raw = {}

        def load_keys(s, u):
            key_raw[s, u] = sbuf("key_raw%d%d" % (s, u), [P, 2, T], F32)
            nc.sync.dma_start(out=key_raw[s, u][:], in_=key_pools[s][:, 2 * u : 2 * u + 2, :])

        load_keys(0, 0)
        slot_weight = []
        for s, row in enumerate([size, rsz]):
            slot_weight.append(sbuf("slot_weight%d" % s, [P, PACK], F32))
            nc.scalar.dma_start(out=slot_weight[s][:], in_=row.rearrange("o (n r) -> (o n) r", r=PACK))
        nc.sync.dma_start(lists[0][:], offs)
        load_keys(0, 1)
        load_keys(1, 0)
        load_keys(1, 1)
        nc.sync.dma_start(lists[1][:], offs2)
        query_raw = sbuf("query_raw", [P, PACK, Q], F32)
        nc.sync.dma_start(out=query_raw[:], in_=query.rearrange("(p t) q -> p t q", t=PACK))
        val_raw = {}
        for s, t in value_planes:
            val_raw[s, t] = sbuf("val_raw%d%d" % (s, t), [P, T], F32)
            nc.sync.dma_start(out=val_raw[s, t][:], in_=val_pools[s][:, t, :])
        own_planes = sbuf("own_planes", [P, PACK, Q], F32)
        nc.sync.dma_start(out=own_planes[:], in_=own.rearrange("(p t) q -> p t q", t=PACK))

        ident = sbuf("ident", [P, P], F32)
        make_identity(nc, ident[:])

        def quantize(name, grouped, width):
            codes = sbuf(name + "_codes", [P, width], U32)
            scales = sbuf(name + "_scales", [P, width], U8)
            nc.vector.quantize_mx(out=codes[:].bitcast(FP8X4), scales=scales[:], in_=grouped)
            return codes, scales

        def turn_slots(turned, source):
            words = source[:].bitcast(F32)
            for u in range(2):
                nc.tensor.transpose(turned(u), words[:, u : SLOTS // 2 : 2], ident[:])

        key_pairs = [sbuf("key_pairs%d" % s, [P, 2, SLOTS], U32) for s in range(POOLS)]
        key_window = {}
        key_grouped = {}

        def cast_keys(s, u):
            key_window[s, u] = sbuf("key_window%d%d" % (s, u), [P, T], U32)
            as_pairs = key_window[s, u][:].bitcast(BF16).rearrange("p (c e) -> p c e", e=2)
            planes = key_raw[s, u][:].rearrange("p e c -> p c e")
            split = VECTOR_CAST_COLUMNS[s]
            nc.vector.tensor_copy(as_pairs[:, :split, :], planes[:, :split, :])
            nc.scalar.activation(as_pairs[:, split:, :], planes[:, split:, :], ACT.Copy)

        def gather_keys(s, u):
            nc.vector.tensor_copy(key_pairs[s][:, u, :], key_window[s, u][:].indirect(lists[s][:]))

        def group_keys(s):
            key_grouped[s] = sbuf("key_grouped%d" % s, [P, SLOTS, 2], I32)
            nc.vector.tensor_copy(key_grouped[s][:], key_pairs[s][:].bitcast(I32).rearrange("p u c -> p c u"))

        scores = {}

        def score(s):
            k_codes, k_scales = quantize("key%d" % s, key_grouped[s][:].rearrange("p c u -> p (c u)").bitcast(BF16), SLOTS)
            for j in range(Q_TILES):
                scores[s, j] = bank("scores%d%d" % (s, j), Q_TILES * s + j, [P, SLOTS])
                cols = slice(j * P, (j + 1) * P)
                nc.tensor.matmul_mx(
                    out=scores[s, j][:],
                    lhsT=q_codes[:, cols].bitcast(FP8X4),
                    lhsT_scale=q_scales[:, cols],
                    rhs=k_codes[:].bitcast(FP8X4),
                    rhs_scale=k_scales[:],
                    start=True,
                    stop=True,
                )

        slot_weight_rows = []

        def spread_slot_weights():
            for s in range(POOLS):
                slot_weight_rows.append(bank("slot_weight_rows%d" % s, SLOT_WEIGHT_BANKS[s], [P, PACK, P]))
                for r in range(PACK):
                    nc.tensor.transpose(slot_weight_rows[s][:, r, :], slot_weight[s][:, r : r + 1].to_broadcast([P, P]), ident[:])

        cast_keys(0, 0)
        gather_keys(0, 0)
        cast_keys(0, 1)
        gather_keys(0, 1)
        group_keys(0)
        cast_keys(1, 0)
        gather_keys(1, 0)
        spread_slot_weights()
        cast_keys(1, 1)
        query_grouped = sbuf("query_grouped", [P, Q, PACK], BF16)
        nc.vector.tensor_copy(
            query_grouped[:].rearrange("p (c i) t -> p c t i", i=RUN), query_raw[:].rearrange("p t (c i) -> p c t i", i=RUN)
        )
        gather_keys(1, 1)
        q_codes, q_scales = quantize("query", query_grouped[:].rearrange("p q t -> p (q t)"), Q)
        score(0)
        group_keys(1)
        score(1)

        neg_scores = {}
        neg_max_first = {}
        neg_max = {}
        for j in range(Q_TILES):
            neg_max_first[j] = sbuf("neg_max_first%d" % j, [P, 1], F32)
            neg_scores[j] = sbuf("neg_scores%d" % j, [P, POOLS, SLOTS], F32)
            nc.vector.tensor_scalar(neg_scores[j][:, 0, :], scores[0, j][:], -1.0, None, ALU.mult, ALU.min, accum_out=neg_max_first[j][:])
            neg_max[j] = sbuf("neg_max%d" % j, [P, 1], F32)
            nc.vector.tensor_scalar(
                neg_scores[j][:, 1, :], scores[1, j][:], -1.0, neg_max_first[j][:], ALU.mult, ALU.min, accum_out=neg_max[j][:]
            )
        exps = {}
        row_sum = {}
        for j in range(Q_TILES):
            row_sum[j] = sbuf("row_sum%d" % j, [P, 1], F32)
            exps[j] = sbuf("exps%d" % j, [P, POOLS, SLOTS], F32)
            nc.scalar.activation(exps[j][:], neg_scores[j][:], ACT.Exp, bias=neg_max[j][:], scale=-1.0, accum_out=row_sum[j][:])

        weights_turned = {}
        for j in range(Q_TILES):
            inverse = sbuf("inverse%d" % j, [P, 1], F32)
            nc.vector.reciprocal(inverse[:], row_sum[j][:])
            for s in range(POOLS):
                weights = sbuf("weights%d%d" % (s, j), [P, SLOTS], BF16)
                nc.vector.scalar_tensor_tensor(
                    weights[:].rearrange("p (n r) -> p n r", r=PACK),
                    exps[j][:, s, :].rearrange("p (n r) -> p n r", r=PACK),
                    inverse[:],
                    slot_weight_rows[s][:].rearrange("p r n -> p n r"),
                    ALU.mult,
                    ALU.mult,
                )
                if j == 0:
                    weights_turned[s] = bank("weights_turned%d" % s, s, [P, 2, Q])
                turn_slots(lambda u: weights_turned[s][:, u, j * P : (j + 1) * P], weights)
        weights_grouped = {}
        for s in range(POOLS):
            weights_grouped[s] = sbuf("weights_grouped%d" % s, [P, Q, 2], F32)
            nc.scalar.copy(weights_grouped[s][:], weights_turned[s][:].rearrange("p u c -> p c u"))
        weights_mx = [
            quantize("weights%d" % s, weights_grouped[s][:].rearrange("p c u -> p (c u)").bitcast(BF16), Q) for s in range(POOLS)
        ]

        vector_gather_reuses = ["key_grouped1", "neg_scores0", "neg_scores1", "exps1", "weights_grouped0"]
        place_of = {plane: (b, i) for b, batch in enumerate(VALUE_BATCHES) for i, plane in enumerate(batch)}
        val_turned = {}
        val_grouped = {}

        def gather_values(number):
            s, t = value_planes[number]
            name = "val_picked%d%d" % (s, t)
            if number < SCALAR_VALUE_PLANES:
                last = number == SCALAR_VALUE_PLANES - 1
                window = sbuf("val_window%d%d" % (s, t), [P, T], BF16, reuses="neg_max_first0" if last else None)
                nc.scalar.activation(window[:], val_raw[s, t][:], ACT.Copy)
                picked = sbuf(name, [P, SLOTS], BF16)
                nc.scalar.activation(picked[:], window[:].indirect(lists[s][:]), ACT.Copy)
            else:
                picked = sbuf(name, [P, SLOTS], BF16, reuses=vector_gather_reuses[number - SCALAR_VALUE_PLANES])
                nc.vector.tensor_copy(picked[:], val_raw[s, t][:].indirect(lists[s][:]))
            b, i = place_of[s, t]
            if i == 0:
                val_turned[b] = bank("val_turned%d" % b, VALUE_BANKS[b % len(VALUE_BANKS)], [P, len(VALUE_BATCHES[b]), 2, P])
            turn_slots(lambda u: val_turned[b][:, i, u, :], picked)

        grouped_reuses = {1: "weights11", 2: "weights01"}

        def group_values(b):
            val_grouped[b] = sbuf("val_grouped%d" % b, [P, len(VALUE_BATCHES[b]), P, 2], F32, reuses=grouped_reuses.get(b))
            nc.scalar.copy(val_grouped[b][:], val_turned[b][:].rearrange("p n u c -> p n c u"))

        for number, plane in enumerate(value_planes):
            earlier_tenant = place_of[plane][0] - len(VALUE_BANKS)
            if earlier_tenant >= 0:
                group_values(earlier_tenant)
            gather_values(number)
        for b in range(len(VALUE_BATCHES) - len(VALUE_BANKS), len(VALUE_BATCHES)):
            group_values(b)
        val_mx = {}
        for b, batch in enumerate(VALUE_BATCHES):
            codes, scales = quantize("val%d" % b, val_grouped[b][:].rearrange("p n c u -> p (n c u)").bitcast(BF16), len(batch) * P)
            for i, plane in enumerate(batch):
                val_mx[plane] = (codes[:, i * P : (i + 1) * P], scales[:, i * P : (i + 1) * P])

        result = sbuf("result", [P, PACK, X], F32)
        masked = {}
        for t in range(PACK):
            acc = bank("acc%d" % t, OUTPUT_BANKS[t], [P, Q])
            for s in range(POOLS):
                nc.tensor.matmul_mx(
                    out=acc[:],
                    lhsT=val_mx[s, t][0].bitcast(FP8X4),
                    lhsT_scale=val_mx[s, t][1],
                    rhs=weights_mx[s][0][:].bitcast(FP8X4),
                    rhs_scale=weights_mx[s][1][:],
                    start=(s == 0),
                    stop=(s == POOLS - 1),
                )
            masked[t] = sbuf("masked%d" % t, [P, Q], F32)
            nc.vector.tensor_tensor(masked[t][:], acc[:], own_planes[:, t, :], ALU.mult)
        for t in range(PACK):
            nc.vector.tensor_reduce(result[:, t, :], masked[t][:].rearrange("p (x h) -> p x h", h=HEADS), AXIS_X, ALU.add)
        nc.sync.dma_start(out=out.rearrange("(p t) x -> p t x", t=PACK), in_=result[:])
